import numpy as np
import ml_dtypes


def mxq(x, axis, fmt="e4m3"):
    dtype, down = {"e4m3": (ml_dtypes.float8_e4m3fn, 7), "e5m2": (ml_dtypes.float8_e5m2, 14)}[fmt]
    v = np.moveaxis(np.asarray(x, np.float32).astype(ml_dtypes.bfloat16).astype(np.float64), axis, -1)
    blocks = v.reshape(v.shape[:-1] + (-1, 32))
    amax = np.abs(blocks).max(-1, keepdims=True)
    byte = np.maximum(np.where(amax > 0, np.frexp(amax)[1] - 1 + 127, 0) - down, 1)
    scale = np.exp2(byte - 127.0)
    codes = (blocks / scale).astype(np.float32).astype(dtype).astype(np.float64)
    return np.moveaxis((codes * scale).reshape(v.shape), -1, axis)


WIDE = False


def mx_kscale(k):
    if not WIDE:
        return np.ones(k)
    levels = np.array([10, -10, 5, -5, 0])
    if k % 512:
        return np.exp2(np.random.permutation(np.resize(levels, k // 32))).repeat(32)
    a = np.empty((k // 512, 16))
    for p in range(k // 512):
        a[p, :8] = np.random.permutation(np.resize(levels, 8))
        for g in range(8):
            far = levels[np.abs(levels - a[p, g]) >= 10]
            a[p, g + 8] = far[np.random.randint(len(far))]
    return np.exp2(a.ravel()).repeat(32)


def f64(x):
    return np.asarray(x).astype(np.float64)


def striped(idx):
    return np.tile(idx.reshape(-1, 16).T, (8, 1)).astype(np.uint16)


def unstriped(offs):
    return offs[:16].T.reshape(-1).astype(np.int64)


E2M1 = np.array([0.0, 0.5, 1.0, 1.5, 2.0, 3.0, 4.0, 6.0, -0.0, -0.5, -1.0, -1.5, -2.0, -3.0, -4.0, -6.0])


def pack_weight(w, fmt):
    k, n = w.shape
    w = f64(np.asarray(w, np.float32).astype(ml_dtypes.bfloat16)).reshape(k // 32, 32, n)
    amax = np.abs(w).max(1)
    if fmt == "e4m3":
        byte = np.frexp(amax)[1] - 1 + 127 - 7
    else:
        mant, ex = np.frexp(amax / 6.0)
        byte = np.where(mant > 0.5, ex, ex - 1) + 127
    byte = np.clip(np.where(amax > 0, byte, 1), 1, 254)
    scaled = (w * np.exp2(127.0 - byte)[:, None, :]).reshape(k, n).astype(np.float32)
    by_word = np.ascontiguousarray(scaled.reshape(k // 512, 128, 4, n).transpose(0, 1, 3, 2))
    if fmt == "e4m3":
        words = by_word.astype(ml_dtypes.float8_e4m3fn).view(np.uint8)
    else:
        c = by_word.astype(ml_dtypes.float4_e2m1fn).view(np.uint8) & 0xF
        words = (c[..., 0::2] | (c[..., 1::2] << 4)).reshape(k // 512, 128, 2 * n)
    return np.ascontiguousarray(words), np.ascontiguousarray(byte.astype(np.uint8).reshape(k // 512, 16, n))


def unpack_weight(words, scales, fmt):
    g, _, n = scales.shape
    words = np.ascontiguousarray(words).reshape(g, 128, n, -1)
    if fmt == "e4m3":
        vals = words.view(ml_dtypes.float8_e4m3fn).astype(np.float64)
    else:
        nib = np.empty((g, 128, n, 4), np.uint8)
        nib[..., 0::2] = words & 0xF
        nib[..., 1::2] = words >> 4
        vals = E2M1[nib]
    vals = vals * np.repeat(np.exp2(scales.astype(np.float64) - 127.0), 8, axis=1)[..., None]
    return vals.transpose(0, 1, 3, 2).reshape(g * 512, n)


def gelu(v):
    return 0.5 * v * (1.0 + np.tanh(np.sqrt(2.0 / np.pi) * (v + 0.044715 * v**3)))


K, T, E, C, H, N = 512, 768, 8, 128, 512, 128
PAD = 32


def by_expert(wq, xq):
    return np.concatenate([wq[e].T @ xq[:, e * C:(e + 1) * C] for e in range(E)], axis=1)


def setup_inputs():
    n = np.random.standard_normal
    s = mx_kscale(K)[:, None]
    u = mx_kscale(H)
    first = np.random.permutation(np.repeat(np.arange(E), T // E))
    second = (first + 1 + np.random.permutation(np.repeat(np.arange(E - 1), -(-T // (E - 1)))[:T])) % E
    while np.bincount(second, minlength=E).max() != T // E:
        load = np.bincount(second, minlength=E); hi, lo = int(load.argmax()), int(load.argmin())
        t = np.flatnonzero((second == hi) & (first != lo))[0]; second[t] = lo
    slot_token = np.empty(E * C, np.int64); pos = np.empty((2, T), np.int64); fill = np.zeros(E, np.int64)
    place = np.stack([np.random.permutation(C) for _ in range(E)])
    for r, deal in enumerate((first, second)):
        for t in np.random.permutation(T):
            e = deal[t]
            if fill[e] < C: j = e * C + place[e, fill[e]]; fill[e] += 1; slot_token[j] = t; pos[r, t] = j
            else: pos[r, t] = E * C + t % PAD
    g = np.random.uniform(0.2, 0.8, T)
    w1 = [pack_weight(m, "e2m1") for m in n((E, K, H)) / np.sqrt(K) / s[None]]
    w3 = [pack_weight(m, "e2m1") for m in n((E, K, H)) / np.sqrt(K) / s[None] * u[None, None, :]]
    w2 = [pack_weight(m, "e2m1") for m in n((E, H, N)) / np.sqrt(H) / u[None, :, None]]
    return {
        "xT": (n((K, T)) * s).astype(np.float32),
        "w1_words": np.stack([m[0] for m in w1]),
        "w1_scales": np.stack([m[1] for m in w1]),
        "w3_words": np.stack([m[0] for m in w3]),
        "w3_scales": np.stack([m[1] for m in w3]),
        "w2_words": np.stack([m[0] for m in w2]),
        "w2_scales": np.stack([m[1] for m in w2]),
        "gate": np.stack([np.tile(g, (N, 1)), np.tile(1.0 - g, (N, 1))]).astype(np.float32),
        "offs": striped(slot_token),
        "pos1": striped(pos[0]),
        "pos2": striped(pos[1]),
    }


def reference(xT, w1_words, w1_scales, w3_words, w3_scales, w2_words, w2_scales, gate, offs, pos1, pos2):
    idx = unstriped(offs)
    w1 = np.stack([unpack_weight(w1_words[e], w1_scales[e], "e2m1") for e in range(E)])
    w3 = np.stack([unpack_weight(w3_words[e], w3_scales[e], "e2m1") for e in range(E)])
    w2 = np.stack([unpack_weight(w2_words[e], w2_scales[e], "e2m1") for e in range(E)])
    xq = mxq(f64(xT)[:, idx], 0, "e4m3")
    h = gelu(by_expert(w1, xq))
    h = h * by_expert(w3, xq)
    y = by_expert(w2, mxq(h, 0, "e4m3"))
    y = np.concatenate([y, np.zeros((N, PAD))], axis=1)
    return f64(gate[0]) * y[:, unstriped(pos1)] + f64(gate[1]) * y[:, unstriped(pos2)]

@@ -1,0 +1,209 @@
+from contextlib import ExitStack
+
+import concourse.mybir as mybir
+from concourse.masks import make_identity
+
+K, T, E, C, H, N = 512, 768, 8, 128, 512, 128
+PAD = 32
+P = 128
+S = E * C
+FLOPS = 2 * S * (2 * K * H + H * N)
+
+F32 = mybir.dt.float32
+BF16 = mybir.dt.bfloat16
+I32 = mybir.dt.int32
+U32 = mybir.dt.uint32
+U16 = mybir.dt.uint16
+U8 = mybir.dt.uint8
+FP8X4 = mybir.dt.float8_e4m3fn_x4
+FP4X4 = mybir.dt.float4_e2m1fn_x4
+GELU = mybir.ActivationFunctionType.Gelu_apprx_tanh
+MULT = mybir.AluOpType.mult
+ADD = mybir.AluOpType.add
+
+X_CHUNKS = (256, 256, 128, 128)
+
+
+def tile_moe_cap2_glu_gelu_kernel(
+    tc, xT, w1_words, w1_scales, w3_words, w3_scales, w2_words, w2_scales, gate, offs, pos1, pos2, out
+):
+    nc = tc.nc
+    with ExitStack() as ctx:
+        held = ctx.enter_context(tc.tile_pool(name="held", bufs=1))
+        ring = ctx.enter_context(tc.tile_pool(name="ring", bufs=3))
+        psum = ctx.enter_context(tc.psum_pool(name="psum", bufs=2))
+
+        offs_t = held.tile([P, S // 16], U16, name="offs_t")
+        pos1_t = held.tile([P, T // 16], U16, name="pos1_t")
+        pos2_t = held.tile([P, T // 16], U16, name="pos2_t")
+
+        warm = held.tile([P, 1], F32, name="warm")
+        nc.vector.memset(warm[:], 0.0)
+        nc.scalar.activation(warm[:], warm[:], GELU)
+        s1 = held.tile([P, E, H], U8, name="s1", align_bytes=64)
+        s3 = held.tile([P, E, H], U8, name="s3", align_bytes=64)
+        s2 = held.tile([P, E, N], U8, name="s2", align_bytes=64)
+        for plane in (s1, s3, s2):
+            nc.vector.memset(plane[:].rearrange("p e n -> p (e n)").bitcast(I32), 0)
+        xs = held.tile([P, T], U8, name="xs", align_bytes=64)
+        nc.gpsimd.memset(xs[:], 0)
+        ident = held.tile([P, P], F32, name="ident")
+        make_identity(nc, ident[:])
+        y = held.tile([P, S + PAD], F32, name="y")
+        nc.gpsimd.memset(y[:, S:], 0.0)
+
+        x_rows = xT.rearrange("(p j) w -> p j w", j=4)
+        raw = []
+        t0 = 0
+        for c, width in enumerate(X_CHUNKS):
+            r = held.tile([P, 4, width], F32, name=f"raw{c}")
+            nc.sync.dma_start(out=r[:], in_=x_rows[:, :, t0 : t0 + width])
+            raw.append(r)
+            t0 += width
+        nc.sync.dma_start(offs_t[:], offs)
+        for plane, scales in ((s1, w1_scales), (s3, w3_scales)):
+            for r in range(4):
+                nc.sync.dma_start(
+                    out=plane[r:P:32].bitcast(I32),
+                    in_=scales.bitcast(I32).rearrange("e s (q r) n -> r q (e s) n", r=4)[r],
+                )
+        w1t, w3t = [], []
+        for g in range(E // 2):
+            for tiles, words, nm in ((w1t, w1_words, "w1"), (w3t, w3_words, "w3")):
+                t = held.tile([P, 2, 2 * H], U8, name=f"{nm}_{g}", align_bytes=64)
+                nc.sync.dma_start(
+                    out=t[:].bitcast(I32),
+                    in_=words.bitcast(I32)[2 * g : 2 * g + 2].rearrange("e s p n -> p (e s) n"),
+                )
+                tiles.append(t)
+            if g == 0:
+                w2t = held.tile([P, E, 2 * N], U8, name="w2t", align_bytes=64)
+                nc.sync.dma_start(out=w2t[:].bitcast(I32), in_=w2_words.bitcast(I32).rearrange("e s p n -> p (e s) n"))
+                for r in range(4):
+                    nc.sync.dma_start(
+                        out=s2[r:P:32].bitcast(I32),
+                        in_=w2_scales.bitcast(I32).rearrange("e s (q r) n -> r q (e s) n", r=4)[r],
+                    )
+        nc.sync.dma_start(pos1_t[:], pos1)
+        nc.sync.dma_start(pos2_t[:], pos2)
+        gates = []
+        for i in range(2):
+            g_t = held.tile([P, T], F32, name=f"gate{i}")
+            nc.sync.dma_start(out=g_t[:], in_=gate[i])
+            gates.append(g_t)
+
+        xq = held.tile([P, T], U32, name="xq", align_bytes=64)
+        t0 = 0
+        for c, width in enumerate(X_CHUNKS):
+            xb = held.tile([P, width, 4], BF16, name=f"xb{c}", align_bytes=64)
+            src = raw[c][:].rearrange("p j w -> p w j")
+            cut = width * 21 // 32
+            nc.vector.tensor_copy(out=xb[:, :cut], in_=src[:, :cut])
+            nc.scalar.copy(out=xb[:, cut:], in_=src[:, cut:])
+            cols = slice(t0, t0 + width)
+            t0 += width
+            nc.vector.quantize_mx(out=xq[:, cols].bitcast(FP8X4), scales=xs[:, cols], in_=xb[:].rearrange("p w j -> p (w j)"))
+
+        gq = held.tile([P, S], U32, name="gq", align_bytes=64)
+        gs = held.tile([P, S], U8, name="gs", align_bytes=64)
+
+        def gather(e0, n):
+            sl = slice(e0 * C, (e0 + n) * C)
+            lst = offs_t[:, e0 * C // 16 : (e0 + n) * C // 16]
+            nc.vector.tensor_copy(gq[:, sl], xq[:].indirect(lst))
+            nc.vector.tensor_copy(gs[:, sl], xs[:].indirect(lst))
+
+        a_t, b_t, h_t, xt_t, hq_t, hs_t, y_t, g_t2, hi_t = {}, {}, {}, {}, {}, {}, {}, {}, {}
+
+        def first(e):
+            sl = slice(e * C, (e + 1) * C)
+            for d, words, plane, nm in ((a_t, w1t, s1, "a"), (b_t, w3t, s3, "b")):
+                d[e] = psum.tile([P, H], F32, name=nm)
+                nc.tensor.matmul_mx(
+                    out=d[e][:],
+                    lhsT=gq[:, sl].bitcast(FP8X4),
+                    lhsT_scale=gs[:, sl],
+                    rhs=words[e // 2][:, e % 2].bitcast(FP4X4),
+                    rhs_scale=plane[:, e],
+                    start=True,
+                    stop=True,
+                )
+
+        def gelu(e):
+            g_t2[e] = ring.tile([P, 2, P, 2], F32, name="g")
+            nc.scalar.activation(g_t2[e][:], a_t[e][:].rearrange("s (p u w) -> s u p w", u=2, w=2), GELU)
+
+        def mul(e):
+            h_t[e] = ring.tile([P, 2, P, 2], BF16, name="h")
+            nc.vector.tensor_tensor(h_t[e][:], b_t[e][:].rearrange("s (p u w) -> s u p w", u=2, w=2), g_t2[e][:], MULT)
+
+        def turn(e):
+            xt_t[e] = psum.tile([P, 2, P], F32, name="xt")
+            words = h_t[e][:].rearrange("s u p w -> s (u p w)").bitcast(F32)
+            for u in range(2):
+                nc.tensor.transpose(xt_t[e][:, u], words[:, u * P : (u + 1) * P], ident[:])
+
+        def lay(e, engine):
+            hi_t[e] = ring.tile([P, C, 4], BF16, name="hi", align_bytes=64)
+            dst = hi_t[e][:].rearrange("p s d -> p (s d)").bitcast(F32).rearrange("p (s u) -> p s u", u=2)
+            srcv = xt_t[e][:].rearrange("p u s -> p s u")
+            if engine == "v":
+                nc.vector.tensor_copy(dst, srcv)
+            else:
+                nc.scalar.copy(dst, srcv)
+
+        def quant(e):
+            hq_t[e] = ring.tile([P, C], U32, name="hq", align_bytes=64)
+            hs_t[e] = ring.tile([P, C], U8, name="hs", align_bytes=64)
+            nc.vector.quantize_mx(out=hq_t[e][:].bitcast(FP8X4), scales=hs_t[e][:], in_=hi_t[e][:].rearrange("p s d -> p (s d)"))
+
+        def second(e):
+            y_t[e] = psum.tile([P, C], F32, name="yp")
+            nc.tensor.matmul_mx(
+                out=y_t[e][:],
+                lhsT=w2t[:, e].bitcast(FP4X4),
+                lhsT_scale=s2[:, e],
+                rhs=hq_t[e][:].bitcast(FP8X4),
+                rhs_scale=hs_t[e][:],
+                start=True,
+                stop=True,
+            )
+
+        def keep(e, engine):
+            dst = y[:, e * C : (e + 1) * C]
+            if engine == "v":
+                nc.vector.tensor_copy(dst, y_t[e][:])
+            else:
+                nc.scalar.copy(dst, y_t[e][:])
+
+        gather(0, 1)
+        gather(1, 1)
+        first(0)
+        ahead = 2
+        for e in range(E + 2):
+            if ahead < E and ahead <= e + 2:
+                gather(ahead, 2)
+                ahead += 2
+            if e < E:
+                gelu(e)
+                mul(e)
+                turn(e)
+            if 0 <= e - 1 < E:
+                lay(e - 1, "v" if e - 1 == E - 1 else "s")
+                quant(e - 1)
+                second(e - 1)
+            if 0 <= e - 2 < E:
+                keep(e - 2, "v" if e - 2 == E - 1 else "s")
+            if e + 1 < E:
+                first(e + 1)
+
+        o1 = held.tile([P, T], F32, name="o1")
+        o2 = held.tile([P, T], F32, name="o2")
+        res = held.tile([P, T], F32, name="res")
+        for lo, hi in ((0, 448), (448, T)):
+            sl = slice(lo, hi)
+            ls = slice(lo // 16, hi // 16)
+            nc.vector.tensor_tensor(o1[:, sl], y[:].indirect(pos1_t[:, ls]), gates[0][:, sl], MULT)
+            nc.vector.tensor_tensor(o2[:, sl], y[:].indirect(pos2_t[:, ls]), gates[1][:, sl], MULT)
+            nc.vector.tensor_tensor(res[:, sl], o1[:, sl], o2[:, sl], ADD)
+            nc.sync.dma_start(out=out[:, sl], in_=res[:, sl])

@@ -31,6 +31,7 @@ def tile_moe_cap2_glu_gelu_kernel(
     with ExitStack() as ctx:
         held = ctx.enter_context(tc.tile_pool(name="held", bufs=1))
         ring = ctx.enter_context(tc.tile_pool(name="ring", bufs=3))
+        pair = ctx.enter_context(tc.tile_pool(name="pair", bufs=2))
         psum = ctx.enter_context(tc.psum_pool(name="psum", bufs=2))
 
         offs_t = held.tile([P, S // 16], U16, name="offs_t")
@@ -38,15 +39,16 @@ def tile_moe_cap2_glu_gelu_kernel(
         pos2_t = held.tile([P, T // 16], U16, name="pos2_t")
 
         warm = held.tile([P, 1], F32, name="warm")
-        nc.vector.memset(warm[:], 0.0)
+        nc.gpsimd.memset(warm[:], 0.0)
         nc.scalar.activation(warm[:], warm[:], GELU)
         s1 = held.tile([P, E, H], U8, name="s1", align_bytes=64)
         s3 = held.tile([P, E, H], U8, name="s3", align_bytes=64)
         s2 = held.tile([P, E, N], U8, name="s2", align_bytes=64)
-        for plane in (s1, s3, s2):
+        for plane in (s1, s3):
             nc.vector.memset(plane[:].rearrange("p e n -> p (e n)").bitcast(I32), 0)
         xs = held.tile([P, T], U8, name="xs", align_bytes=64)
         nc.gpsimd.memset(xs[:], 0)
+        nc.gpsimd.memset(s2[:].rearrange("p e n -> p (e n)").bitcast(I32), 0)
         ident = held.tile([P, P], F32, name="ident")
         make_identity(nc, ident[:])
         y = held.tile([P, S + PAD], F32, name="y")
@@ -104,25 +106,27 @@ def tile_moe_cap2_glu_gelu_kernel(
             t0 += width
             nc.vector.quantize_mx(out=xq[:, cols].bitcast(FP8X4), scales=xs[:, cols], in_=xb[:].rearrange("p w j -> p (w j)"))
 
-        gq = held.tile([P, S], U32, name="gq", align_bytes=64)
-        gs = held.tile([P, S], U8, name="gs", align_bytes=64)
+        gq, gs = {}, {}
 
         def gather(e0, n):
-            sl = slice(e0 * C, (e0 + n) * C)
+            if e0 % 2 == 0:
+                gq[e0 // 2] = pair.tile([P, 2 * C], U32, name="gq", align_bytes=64)
+                gs[e0 // 2] = pair.tile([P, 2 * C], U8, name="gs", align_bytes=64)
+            sl = slice(e0 % 2 * C, (e0 % 2 + n) * C)
             lst = offs_t[:, e0 * C // 16 : (e0 + n) * C // 16]
-            nc.vector.tensor_copy(gq[:, sl], xq[:].indirect(lst))
-            nc.vector.tensor_copy(gs[:, sl], xs[:].indirect(lst))
+            nc.vector.tensor_copy(gq[e0 // 2][:, sl], xq[:].indirect(lst))
+            nc.vector.tensor_copy(gs[e0 // 2][:, sl], xs[:].indirect(lst))
 
         a_t, b_t, h_t, xt_t, hq_t, hs_t, y_t, g_t2, hi_t = {}, {}, {}, {}, {}, {}, {}, {}, {}
 
         def first(e):
-            sl = slice(e * C, (e + 1) * C)
+            sl = slice(e % 2 * C, (e % 2 + 1) * C)
             for d, words, plane, nm in ((a_t, w1t, s1, "a"), (b_t, w3t, s3, "b")):
                 d[e] = psum.tile([P, H], F32, name=nm)
                 nc.tensor.matmul_mx(
                     out=d[e][:],
-                    lhsT=gq[:, sl].bitcast(FP8X4),
-                    lhsT_scale=gs[:, sl],
+                    lhsT=gq[e // 2][:, sl].bitcast(FP8X4),
+                    lhsT_scale=gs[e // 2][:, sl],
                     rhs=words[e // 2][:, e % 2].bitcast(FP4X4),
                     rhs_scale=plane[:, e],
                     start=True,
@@ -133,9 +137,12 @@ def tile_moe_cap2_glu_gelu_kernel(
             g_t2[e] = ring.tile([P, 2, P, 2], F32, name="g")
             nc.scalar.activation(g_t2[e][:], a_t[e][:].rearrange("s (p u w) -> s u p w", u=2, w=2), GELU)
 
-        def mul(e):
+        def mul(e, halves=1):
             h_t[e] = ring.tile([P, 2, P, 2], BF16, name="h")
-            nc.vector.tensor_tensor(h_t[e][:], b_t[e][:].rearrange("s (p u w) -> s u p w", u=2, w=2), g_t2[e][:], MULT)
+            b = b_t[e][:].rearrange("s (p u w) -> s u p w", u=2, w=2)
+            for i in range(halves):
+                us = slice(i * 2 // halves, (i + 1) * 2 // halves)
+                nc.vector.tensor_tensor(h_t[e][:, us], b[:, us], g_t2[e][:, us], MULT)
 
         def turn(e):
             xt_t[e] = psum.tile([P, 2, P], F32, name="xt")
@@ -186,7 +193,7 @@ def tile_moe_cap2_glu_gelu_kernel(
                 ahead += 2
             if e < E:
                 gelu(e)
-                mul(e)
+                mul(e, 2 if e == E - 1 else 1)
                 turn(e)
             if 0 <= e - 1 < E:
                 lay(e - 1, "v" if e - 1 == E - 1 else "s")
@@ -200,7 +207,7 @@ def tile_moe_cap2_glu_gelu_kernel(
         o1 = held.tile([P, T], F32, name="o1")
         o2 = held.tile([P, T], F32, name="o2")
         res = held.tile([P, T], F32, name="res")
-        for lo, hi in ((0, 448), (448, T)):
+        for lo, hi in ((0, 512), (512, T)):
             sl = slice(lo, hi)
             ls = slice(lo // 16, hi // 16)
             nc.vector.tensor_tensor(o1[:, sl], y[:].indirect(pos1_t[:, ls]), gates[0][:, sl], MULT)

@@ -21,7 +21,7 @@ GELU = mybir.ActivationFunctionType.Gelu_apprx_tanh
 MULT = mybir.AluOpType.mult
 ADD = mybir.AluOpType.add
 
-X_CHUNKS = (256, 256, 128, 128)
+X_CHUNKS = (256, 256, 256)
 
 
 def tile_moe_cap2_glu_gelu_kernel(
@@ -39,53 +39,59 @@ def tile_moe_cap2_glu_gelu_kernel(
         pos2_t = held.tile([P, T // 16], U16, name="pos2_t")
 
         warm = held.tile([P, 1], F32, name="warm")
-        nc.gpsimd.memset(warm[:], 0.0)
-        nc.scalar.activation(warm[:], warm[:], GELU)
         s1 = held.tile([P, E, H], U8, name="s1", align_bytes=64)
         s3 = held.tile([P, E, H], U8, name="s3", align_bytes=64)
         s2 = held.tile([P, E, N], U8, name="s2", align_bytes=64)
-        for plane in (s1, s3):
-            nc.vector.memset(plane[:].rearrange("p e n -> p (e n)").bitcast(I32), 0)
         xs = held.tile([P, T], U8, name="xs", align_bytes=64)
-        nc.gpsimd.memset(xs[:], 0)
-        nc.gpsimd.memset(s2[:].rearrange("p e n -> p (e n)").bitcast(I32), 0)
+        words = []
+        for g in range(E // 2):
+            w = held.tile([P, 2, 2, 2 * H], U8, name=f"words{g}", align_bytes=64)
+            words.append(w)
+        nc.vector.memset(warm[:], 0.0)
+        nc.scalar.activation(warm[:], warm[:], GELU)
+        for plane in (s3, s1, s2):
+            nc.vector.memset(plane[:].rearrange("p e n -> p (e n)").bitcast(I32), 0)
+        nc.vector.memset(xs[:].bitcast(I32), 0)
+        for g in range(2):
+            nc.vector.memset(words[g][:].bitcast(I32)[:, :, 0, 0:1], 0)
+
         ident = held.tile([P, P], F32, name="ident")
         make_identity(nc, ident[:])
         y = held.tile([P, S + PAD], F32, name="y")
         nc.gpsimd.memset(y[:, S:], 0.0)
 
-        x_rows = xT.rearrange("(p j) w -> p j w", j=4)
         raw = []
         t0 = 0
         for c, width in enumerate(X_CHUNKS):
             r = held.tile([P, 4, width], F32, name=f"raw{c}")
-            nc.sync.dma_start(out=r[:], in_=x_rows[:, :, t0 : t0 + width])
+            nc.sync.dma_start(out=r[:], in_=xT.rearrange("(p j) w -> p j w", j=4)[:, :, t0 : t0 + width])
             raw.append(r)
             t0 += width
         nc.sync.dma_start(offs_t[:], offs)
-        for plane, scales in ((s1, w1_scales), (s3, w3_scales)):
+
+        def load_scales(queue, plane, scales):
             for r in range(4):
-                nc.sync.dma_start(
+                queue.dma_start(
                     out=plane[r:P:32].bitcast(I32),
                     in_=scales.bitcast(I32).rearrange("e s (q r) n -> r q (e s) n", r=4)[r],
                 )
-        w1t, w3t = [], []
-        for g in range(E // 2):
-            for tiles, words, nm in ((w1t, w1_words, "w1"), (w3t, w3_words, "w3")):
-                t = held.tile([P, 2, 2 * H], U8, name=f"{nm}_{g}", align_bytes=64)
+
+        def load_words(g):
+            for i, hbm in enumerate((w1_words, w3_words)):
                 nc.sync.dma_start(
-                    out=t[:].bitcast(I32),
-                    in_=words.bitcast(I32)[2 * g : 2 * g + 2].rearrange("e s p n -> p (e s) n"),
+                    out=words[g][:, i].bitcast(I32),
+                    in_=hbm.bitcast(I32)[2 * g : 2 * g + 2].rearrange("e s p n -> p (e s) n"),
                 )
-                tiles.append(t)
-            if g == 0:
-                w2t = held.tile([P, E, 2 * N], U8, name="w2t", align_bytes=64)
-                nc.sync.dma_start(out=w2t[:].bitcast(I32), in_=w2_words.bitcast(I32).rearrange("e s p n -> p (e s) n"))
-                for r in range(4):
-                    nc.sync.dma_start(
-                        out=s2[r:P:32].bitcast(I32),
-                        in_=w2_scales.bitcast(I32).rearrange("e s (q r) n -> r q (e s) n", r=4)[r],
-                    )
+
+        load_scales(nc.gpsimd, s3, w3_scales)
+        load_scales(nc.sync, s1, w1_scales)
+        load_words(0)
+        load_words(1)
+        w2t = held.tile([P, E, 2 * N], U8, name="w2t", align_bytes=64)
+        nc.sync.dma_start(out=w2t[:].bitcast(I32), in_=w2_words.bitcast(I32).rearrange("e s p n -> p (e s) n"))
+        load_scales(nc.sync, s2, w2_scales)
+        load_words(2)
+        load_words(3)
         nc.sync.dma_start(pos1_t[:], pos1)
         nc.sync.dma_start(pos2_t[:], pos2)
         gates = []
@@ -121,13 +127,13 @@ def tile_moe_cap2_glu_gelu_kernel(
 
         def first(e):
             sl = slice(e % 2 * C, (e % 2 + 1) * C)
-            for d, words, plane, nm in ((a_t, w1t, s1, "a"), (b_t, w3t, s3, "b")):
+            for i, (d, plane, nm) in enumerate(((a_t, s1, "a"), (b_t, s3, "b"))):
                 d[e] = psum.tile([P, H], F32, name=nm)
                 nc.tensor.matmul_mx(
                     out=d[e][:],
                     lhsT=gq[e // 2][:, sl].bitcast(FP8X4),
                     lhsT_scale=gs[e // 2][:, sl],
-                    rhs=words[e // 2][:, e % 2].bitcast(FP4X4),
+                    rhs=words[e // 2][:, i, e % 2].bitcast(FP4X4),
                     rhs_scale=plane[:, e],
                     start=True,
                     stop=True,
@@ -146,9 +152,9 @@ def tile_moe_cap2_glu_gelu_kernel(
 
         def turn(e):
             xt_t[e] = psum.tile([P, 2, P], F32, name="xt")
-            words = h_t[e][:].rearrange("s u p w -> s (u p w)").bitcast(F32)
+            pairs = h_t[e][:].rearrange("s u p w -> s (u p w)").bitcast(F32)
             for u in range(2):
-                nc.tensor.transpose(xt_t[e][:, u], words[:, u * P : (u + 1) * P], ident[:])
+                nc.tensor.transpose(xt_t[e][:, u], pairs[:, u * P : (u + 1) * P], ident[:])
 
         def lay(e, engine):
             hi_t[e] = ring.tile([P, C, 4], BF16, name="hi", align_bytes=64)

@@ -7,6 +7,7 @@ K, T, E, C, H, N = 512, 768, 8, 128, 512, 128
 PAD = 32
 P = 128
 S = E * C
+GPSIMD_EXPERTS = (2, 5)
 FLOPS = 2 * S * (2 * K * H + H * N)
 
 F32 = mybir.dt.float32
@@ -143,12 +144,19 @@ def tile_moe_cap2_glu_gelu_kernel(
             g_t2[e] = ring.tile([P, 2, P, 2], F32, name="g")
             nc.scalar.activation(g_t2[e][:], a_t[e][:].rearrange("s (p u w) -> s u p w", u=2, w=2), GELU)
 
-        def mul(e, halves=1):
+        def mul(e):
             h_t[e] = ring.tile([P, 2, P, 2], BF16, name="h")
             b = b_t[e][:].rearrange("s (p u w) -> s u p w", u=2, w=2)
-            for i in range(halves):
-                us = slice(i * 2 // halves, (i + 1) * 2 // halves)
-                nc.vector.tensor_tensor(h_t[e][:, us], b[:, us], g_t2[e][:, us], MULT)
+            if e in GPSIMD_EXPERTS:
+                bs = ring.tile([P, 2, P, 2], F32, name="bs")
+                nc.scalar.copy(bs[:], b)
+                for u in range(2):
+                    nc.gpsimd.tensor_tensor(h_t[e][:, u], bs[:, u], g_t2[e][:, u], MULT)
+            elif e == E - 1:
+                for u in range(2):
+                    nc.vector.tensor_tensor(h_t[e][:, u], b[:, u], g_t2[e][:, u], MULT)
+            else:
+                nc.vector.tensor_tensor(h_t[e][:], b, g_t2[e][:], MULT)
 
         def turn(e):
             xt_t[e] = psum.tile([P, 2, P], F32, name="xt")
@@ -156,14 +164,11 @@ def tile_moe_cap2_glu_gelu_kernel(
             for u in range(2):
                 nc.tensor.transpose(xt_t[e][:, u], pairs[:, u * P : (u + 1) * P], ident[:])
 
-        def lay(e, engine):
+        def lay(e):
             hi_t[e] = ring.tile([P, C, 4], BF16, name="hi", align_bytes=64)
             dst = hi_t[e][:].rearrange("p s d -> p (s d)").bitcast(F32).rearrange("p (s u) -> p s u", u=2)
             srcv = xt_t[e][:].rearrange("p u s -> p s u")
-            if engine == "v":
-                nc.vector.tensor_copy(dst, srcv)
-            else:
-                nc.scalar.copy(dst, srcv)
+            nc.scalar.copy(dst, srcv)
 
         def quant(e):
             hq_t[e] = ring.tile([P, C], U32, name="hq", align_bytes=64)
@@ -182,12 +187,8 @@ def tile_moe_cap2_glu_gelu_kernel(
                 stop=True,
             )
 
-        def keep(e, engine):
-            dst = y[:, e * C : (e + 1) * C]
-            if engine == "v":
-                nc.vector.tensor_copy(dst, y_t[e][:])
-            else:
-                nc.scalar.copy(dst, y_t[e][:])
+        def keep(e):
+            nc.scalar.copy(y[:, e * C : (e + 1) * C], y_t[e][:])
 
         gather(0, 1)
         gather(1, 1)
@@ -199,24 +200,26 @@ def tile_moe_cap2_glu_gelu_kernel(
                 ahead += 2
             if e < E:
                 gelu(e)
-                mul(e, 2 if e == E - 1 else 1)
+                mul(e)
                 turn(e)
             if 0 <= e - 1 < E:
-                lay(e - 1, "v" if e - 1 == E - 1 else "s")
+                lay(e - 1)
                 quant(e - 1)
                 second(e - 1)
             if 0 <= e - 2 < E:
-                keep(e - 2, "v" if e - 2 == E - 1 else "s")
+                keep(e - 2)
             if e + 1 < E:
                 first(e + 1)
 
         o1 = held.tile([P, T], F32, name="o1")
         o2 = held.tile([P, T], F32, name="o2")
         res = held.tile([P, T], F32, name="res")
-        for lo, hi in ((0, 512), (512, T)):
-            sl = slice(lo, hi)
-            ls = slice(lo // 16, hi // 16)
+        parts = ((0, 512), (512, T))
+        for lo, hi in parts:
+            sl, ls = slice(lo, hi), slice(lo // 16, hi // 16)
             nc.vector.tensor_tensor(o1[:, sl], y[:].indirect(pos1_t[:, ls]), gates[0][:, sl], MULT)
             nc.vector.tensor_tensor(o2[:, sl], y[:].indirect(pos2_t[:, ls]), gates[1][:, sl], MULT)
+        for lo, hi in parts:
+            sl = slice(lo, hi)
             nc.vector.tensor_tensor(res[:, sl], o1[:, sl], o2[:, sl], ADD)
             nc.sync.dma_start(out=out[:, sl], in_=res[:, sl])

@@ -7,7 +7,8 @@ K, T, E, C, H, N = 512, 768, 8, 128, 512, 128
 PAD = 32
 P = 128
 S = E * C
-GPSIMD_EXPERTS = (2, 5)
+WARM_PASSES = 10
+GPSIMD_EXPERTS = ()
 FLOPS = 2 * S * (2 * K * H + H * N)
 
 F32 = mybir.dt.float32
@@ -23,6 +24,7 @@ MULT = mybir.AluOpType.mult
 ADD = mybir.AluOpType.add
 
 X_CHUNKS = (256, 256, 256)
+X_BLOCKS = ((256,), (256,), (128, 128))
 
 
 def tile_moe_cap2_glu_gelu_kernel(
@@ -44,35 +46,46 @@ def tile_moe_cap2_glu_gelu_kernel(
         s3 = held.tile([P, E, H], U8, name="s3", align_bytes=64)
         s2 = held.tile([P, E, N], U8, name="s2", align_bytes=64)
         xs = held.tile([P, T], U8, name="xs", align_bytes=64)
-        words = []
+        w2t = held.tile([P, E, 2 * N], U8, name="w2t", align_bytes=64)
+        words, raw, gates = [], [], []
         for g in range(E // 2):
             w = held.tile([P, 2, 2, 2 * H], U8, name=f"words{g}", align_bytes=64)
             words.append(w)
+        for c, width in enumerate(X_CHUNKS):
+            r = held.tile([P, 4, width], F32, name=f"raw{c}")
+            raw.append(r)
+        for i in range(2):
+            g_t = held.tile([P, T], F32, name=f"gate{i}")
+            gates.append(g_t)
+
+        def zero(bytes_3d):
+            nc.vector.memset(bytes_3d.rearrange("p e n -> p (e n)").bitcast(I32), 0)
+
         nc.vector.memset(warm[:], 0.0)
         nc.scalar.activation(warm[:], warm[:], GELU)
-        for plane in (s3, s1, s2):
-            nc.vector.memset(plane[:].rearrange("p e n -> p (e n)").bitcast(I32), 0)
+        zero(s1[:])
+        zero(s3[:])
         nc.vector.memset(xs[:].bitcast(I32), 0)
-        for g in range(2):
-            nc.vector.memset(words[g][:].bitcast(I32)[:, :, 0, 0:1], 0)
-
+        zero(s2[:])
+        idle = held.tile([P, 4 * P], BF16, name="idle", align_bytes=64)
+        idle_q = held.tile([P, P], U32, name="idle_q", align_bytes=64)
+        idle_s = held.tile([P, P], U8, name="idle_s", align_bytes=64)
+        nc.vector.memset(idle[:], 0.0)
+        nc.vector.quantize_mx(out=idle_q[:].bitcast(FP8X4), scales=idle_s[:], in_=idle[:])
         ident = held.tile([P, P], F32, name="ident")
         make_identity(nc, ident[:])
         y = held.tile([P, S + PAD], F32, name="y")
         nc.gpsimd.memset(y[:, S:], 0.0)
 
-        raw = []
-        t0 = 0
-        for c, width in enumerate(X_CHUNKS):
-            r = held.tile([P, 4, width], F32, name=f"raw{c}")
-            nc.sync.dma_start(out=r[:], in_=xT.rearrange("(p j) w -> p j w", j=4)[:, :, t0 : t0 + width])
-            raw.append(r)
-            t0 += width
-        nc.sync.dma_start(offs_t[:], offs)
+        def load_x(c):
+            t0 = sum(X_CHUNKS[:c])
+            nc.sync.dma_start(
+                out=raw[c][:], in_=xT.rearrange("(p j) w -> p j w", j=4)[:, :, t0 : t0 + X_CHUNKS[c]]
+            )
 
-        def load_scales(queue, plane, scales):
+        def load_scales(plane, scales):
             for r in range(4):
-                queue.dma_start(
+                nc.sync.dma_start(
                     out=plane[r:P:32].bitcast(I32),
                     in_=scales.bitcast(I32).rearrange("e s (q r) n -> r q (e s) n", r=4)[r],
                 )
@@ -84,34 +97,54 @@ def tile_moe_cap2_glu_gelu_kernel(
                     in_=hbm.bitcast(I32)[2 * g : 2 * g + 2].rearrange("e s p n -> p (e s) n"),
                 )
 
-        load_scales(nc.gpsimd, s3, w3_scales)
-        load_scales(nc.sync, s1, w1_scales)
+        for c in range(len(X_CHUNKS)):
+            load_x(c)
+        nc.sync.dma_start(offs_t[:], offs)
+        load_scales(s1, w1_scales)
         load_words(0)
+        load_scales(s3, w3_scales)
         load_words(1)
-        w2t = held.tile([P, E, 2 * N], U8, name="w2t", align_bytes=64)
         nc.sync.dma_start(out=w2t[:].bitcast(I32), in_=w2_words.bitcast(I32).rearrange("e s p n -> p (e s) n"))
-        load_scales(nc.sync, s2, w2_scales)
+        load_scales(s2, w2_scales)
         load_words(2)
         load_words(3)
         nc.sync.dma_start(pos1_t[:], pos1)
         nc.sync.dma_start(pos2_t[:], pos2)
-        gates = []
         for i in range(2):
-            g_t = held.tile([P, T], F32, name=f"gate{i}")
-            nc.sync.dma_start(out=g_t[:], in_=gate[i])
-            gates.append(g_t)
+            nc.sync.dma_start(out=gates[i][:], in_=gate[i])
+
+        idle_p = psum.tile([P, P], F32, name="yp")
+        for i in range(WARM_PASSES):
+            nc.tensor.matmul_mx(
+                out=idle_p[:],
+                lhsT=s1[:, 0, : 2 * P].bitcast(FP4X4),
+                lhsT_scale=s1[:, 1, :P],
+                rhs=idle_q[:].bitcast(FP8X4),
+                rhs_scale=idle_s[:],
+                start=True,
+                stop=True,
+            )
 
         xq = held.tile([P, T], U32, name="xq", align_bytes=64)
         t0 = 0
-        for c, width in enumerate(X_CHUNKS):
-            xb = held.tile([P, width, 4], BF16, name=f"xb{c}", align_bytes=64)
-            src = raw[c][:].rearrange("p j w -> p w j")
-            cut = width * 21 // 32
-            nc.vector.tensor_copy(out=xb[:, :cut], in_=src[:, :cut])
-            nc.scalar.copy(out=xb[:, cut:], in_=src[:, cut:])
-            cols = slice(t0, t0 + width)
-            t0 += width
-            nc.vector.quantize_mx(out=xq[:, cols].bitcast(FP8X4), scales=xs[:, cols], in_=xb[:].rearrange("p w j -> p (w j)"))
+        for c, widths in enumerate(X_BLOCKS):
+            xb = held.tile([P, X_CHUNKS[c], 4], BF16, name=f"xb{c}", align_bytes=64)
+            lo = 0
+            for width in widths:
+                hi, cut = lo + width, lo + width * 21 // 128 * 4
+                src = raw[c][:].rearrange("p j w -> p w j")
+                nc.vector.tensor_copy(out=xb[:, lo:cut], in_=src[:, lo:cut])
+                nc.scalar.copy(out=xb[:, cut:hi], in_=src[:, cut:hi])
+                lo = hi
+            lo = 0
+            for width in widths:
+                cols = slice(t0, t0 + width)
+                nc.vector.quantize_mx(
+                    out=xq[:, cols].bitcast(FP8X4),
+                    scales=xs[:, cols],
+                    in_=xb[:, lo : lo + width].rearrange("p w j -> p (w j)"),
+                )
+                lo, t0 = lo + width, t0 + width
 
         gq, gs = {}, {}
 
@@ -190,14 +223,13 @@ def tile_moe_cap2_glu_gelu_kernel(
         def keep(e):
             nc.scalar.copy(y[:, e * C : (e + 1) * C], y_t[e][:])
 
-        gather(0, 1)
-        gather(1, 1)
+        groups = [(0, 1), (1, 1), (2, 2), (4, 2), (6, 2)]
+        gather(*groups.pop(0))
+        gather(*groups.pop(0))
         first(0)
-        ahead = 2
         for e in range(E + 2):
-            if ahead < E and ahead <= e + 2:
-                gather(ahead, 2)
-                ahead += 2
+            if groups and groups[0][0] <= e + 2:
+                gather(*groups.pop(0))
             if e < E:
                 gelu(e)
                 mul(e)

from contextlib import ExitStack

import concourse.mybir as mybir
from concourse.masks import make_identity

K, T, E, C, H, N = 512, 768, 8, 128, 512, 128
PAD = 32
P = 128
S = E * C
WARM_PASSES = 10
GPSIMD_EXPERTS = ()
FLOPS = 2 * S * (2 * K * H + H * N)

F32 = mybir.dt.float32
BF16 = mybir.dt.bfloat16
I32 = mybir.dt.int32
U32 = mybir.dt.uint32
U16 = mybir.dt.uint16
U8 = mybir.dt.uint8
FP8X4 = mybir.dt.float8_e4m3fn_x4
FP4X4 = mybir.dt.float4_e2m1fn_x4
GELU = mybir.ActivationFunctionType.Gelu_apprx_tanh
MULT = mybir.AluOpType.mult
ADD = mybir.AluOpType.add

X_CHUNKS = (256, 256, 256)
X_BLOCKS = ((256,), (256,), (128, 128))


def tile_moe_cap2_glu_gelu_kernel(
    tc, xT, w1_words, w1_scales, w3_words, w3_scales, w2_words, w2_scales, gate, offs, pos1, pos2, out
):
    nc = tc.nc
    with ExitStack() as ctx:
        held = ctx.enter_context(tc.tile_pool(name="held", bufs=1))
        ring = ctx.enter_context(tc.tile_pool(name="ring", bufs=3))
        pair = ctx.enter_context(tc.tile_pool(name="pair", bufs=2))
        psum = ctx.enter_context(tc.psum_pool(name="psum", bufs=2))

        offs_t = held.tile([P, S // 16], U16, name="offs_t")
        pos1_t = held.tile([P, T // 16], U16, name="pos1_t")
        pos2_t = held.tile([P, T // 16], U16, name="pos2_t")

        warm = held.tile([P, 1], F32, name="warm")
        s1 = held.tile([P, E, H], U8, name="s1", align_bytes=64)
        s3 = held.tile([P, E, H], U8, name="s3", align_bytes=64)
        s2 = held.tile([P, E, N], U8, name="s2", align_bytes=64)
        xs = held.tile([P, T], U8, name="xs", align_bytes=64)
        w2t = held.tile([P, E, 2 * N], U8, name="w2t", align_bytes=64)
        words, raw, gates = [], [], []
        for g in range(E // 2):
            w = held.tile([P, 2, 2, 2 * H], U8, name=f"words{g}", align_bytes=64)
            words.append(w)
        for c, width in enumerate(X_CHUNKS):
            r = held.tile([P, 4, width], F32, name=f"raw{c}")
            raw.append(r)
        for i in range(2):
            g_t = held.tile([P, T], F32, name=f"gate{i}")
            gates.append(g_t)

        def zero(bytes_3d):
            nc.vector.memset(bytes_3d.rearrange("p e n -> p (e n)").bitcast(I32), 0)

        nc.vector.memset(warm[:], 0.0)
        nc.scalar.activation(warm[:], warm[:], GELU)
        zero(s1[:])
        zero(s3[:])
        nc.vector.memset(xs[:].bitcast(I32), 0)
        zero(s2[:])
        idle = held.tile([P, 4 * P], BF16, name="idle", align_bytes=64)
        idle_q = held.tile([P, P], U32, name="idle_q", align_bytes=64)
        idle_s = held.tile([P, P], U8, name="idle_s", align_bytes=64)
        nc.vector.memset(idle[:], 0.0)
        nc.vector.quantize_mx(out=idle_q[:].bitcast(FP8X4), scales=idle_s[:], in_=idle[:])
        ident = held.tile([P, P], F32, name="ident")
        make_identity(nc, ident[:])
        y = held.tile([P, S + PAD], F32, name="y")
        nc.gpsimd.memset(y[:, S:], 0.0)

        def load_x(c):
            t0 = sum(X_CHUNKS[:c])
            nc.sync.dma_start(
                out=raw[c][:], in_=xT.rearrange("(p j) w -> p j w", j=4)[:, :, t0 : t0 + X_CHUNKS[c]]
            )

        def load_scales(plane, scales):
            for r in range(4):
                nc.sync.dma_start(
                    out=plane[r:P:32].bitcast(I32),
                    in_=scales.bitcast(I32).rearrange("e s (q r) n -> r q (e s) n", r=4)[r],
                )

        def load_words(g):
            for i, hbm in enumerate((w1_words, w3_words)):
                nc.sync.dma_start(
                    out=words[g][:, i].bitcast(I32),
                    in_=hbm.bitcast(I32)[2 * g : 2 * g + 2].rearrange("e s p n -> p (e s) n"),
                )

        for c in range(len(X_CHUNKS)):
            load_x(c)
        nc.sync.dma_start(offs_t[:], offs)
        load_scales(s1, w1_scales)
        load_words(0)
        load_scales(s3, w3_scales)
        load_words(1)
        nc.sync.dma_start(out=w2t[:].bitcast(I32), in_=w2_words.bitcast(I32).rearrange("e s p n -> p (e s) n"))
        load_scales(s2, w2_scales)
        load_words(2)
        load_words(3)
        nc.sync.dma_start(pos1_t[:], pos1)
        nc.sync.dma_start(pos2_t[:], pos2)
        for i in range(2):
            nc.sync.dma_start(out=gates[i][:], in_=gate[i])

        idle_p = psum.tile([P, P], F32, name="yp")
        for i in range(WARM_PASSES):
            nc.tensor.matmul_mx(
                out=idle_p[:],
                lhsT=s1[:, 0, : 2 * P].bitcast(FP4X4),
                lhsT_scale=s1[:, 1, :P],
                rhs=idle_q[:].bitcast(FP8X4),
                rhs_scale=idle_s[:],
                start=True,
                stop=True,
            )

        xq = held.tile([P, T], U32, name="xq", align_bytes=64)
        t0 = 0
        for c, widths in enumerate(X_BLOCKS):
            xb = held.tile([P, X_CHUNKS[c], 4], BF16, name=f"xb{c}", align_bytes=64)
            lo = 0
            for width in widths:
                hi, cut = lo + width, lo + width * 21 // 128 * 4
                src = raw[c][:].rearrange("p j w -> p w j")
                nc.vector.tensor_copy(out=xb[:, lo:cut], in_=src[:, lo:cut])
                nc.scalar.copy(out=xb[:, cut:hi], in_=src[:, cut:hi])
                lo = hi
            lo = 0
            for width in widths:
                cols = slice(t0, t0 + width)
                nc.vector.quantize_mx(
                    out=xq[:, cols].bitcast(FP8X4),
                    scales=xs[:, cols],
                    in_=xb[:, lo : lo + width].rearrange("p w j -> p (w j)"),
                )
                lo, t0 = lo + width, t0 + width

        gq, gs = {}, {}

        def gather(e0, n):
            if e0 % 2 == 0:
                gq[e0 // 2] = pair.tile([P, 2 * C], U32, name="gq", align_bytes=64)
                gs[e0 // 2] = pair.tile([P, 2 * C], U8, name="gs", align_bytes=64)
            sl = slice(e0 % 2 * C, (e0 % 2 + n) * C)
            lst = offs_t[:, e0 * C // 16 : (e0 + n) * C // 16]
            nc.vector.tensor_copy(gq[e0 // 2][:, sl], xq[:].indirect(lst))
            nc.vector.tensor_copy(gs[e0 // 2][:, sl], xs[:].indirect(lst))

        a_t, b_t, h_t, xt_t, hq_t, hs_t, y_t, g_t2, hi_t = {}, {}, {}, {}, {}, {}, {}, {}, {}

        def first(e):
            sl = slice(e % 2 * C, (e % 2 + 1) * C)
            for i, (d, plane, nm) in enumerate(((a_t, s1, "a"), (b_t, s3, "b"))):
                d[e] = psum.tile([P, H], F32, name=nm)
                nc.tensor.matmul_mx(
                    out=d[e][:],
                    lhsT=gq[e // 2][:, sl].bitcast(FP8X4),
                    lhsT_scale=gs[e // 2][:, sl],
                    rhs=words[e // 2][:, i, e % 2].bitcast(FP4X4),
                    rhs_scale=plane[:, e],
                    start=True,
                    stop=True,
                )

        def gelu(e):
            g_t2[e] = ring.tile([P, 2, P, 2], F32, name="g")
            nc.scalar.activation(g_t2[e][:], a_t[e][:].rearrange("s (p u w) -> s u p w", u=2, w=2), GELU)

        def mul(e):
            h_t[e] = ring.tile([P, 2, P, 2], BF16, name="h")
            b = b_t[e][:].rearrange("s (p u w) -> s u p w", u=2, w=2)
            if e in GPSIMD_EXPERTS:
                bs = ring.tile([P, 2, P, 2], F32, name="bs")
                nc.scalar.copy(bs[:], b)
                for u in range(2):
                    nc.gpsimd.tensor_tensor(h_t[e][:, u], bs[:, u], g_t2[e][:, u], MULT)
            elif e == E - 1:
                for u in range(2):
                    nc.vector.tensor_tensor(h_t[e][:, u], b[:, u], g_t2[e][:, u], MULT)
            else:
                nc.vector.tensor_tensor(h_t[e][:], b, g_t2[e][:], MULT)

        def turn(e):
            xt_t[e] = psum.tile([P, 2, P], F32, name="xt")
            pairs = h_t[e][:].rearrange("s u p w -> s (u p w)").bitcast(F32)
            for u in range(2):
                nc.tensor.transpose(xt_t[e][:, u], pairs[:, u * P : (u + 1) * P], ident[:])

        def lay(e):
            hi_t[e] = ring.tile([P, C, 4], BF16, name="hi", align_bytes=64)
            dst = hi_t[e][:].rearrange("p s d -> p (s d)").bitcast(F32).rearrange("p (s u) -> p s u", u=2)
            srcv = xt_t[e][:].rearrange("p u s -> p s u")
            nc.scalar.copy(dst, srcv)

        def quant(e):
            hq_t[e] = ring.tile([P, C], U32, name="hq", align_bytes=64)
            hs_t[e] = ring.tile([P, C], U8, name="hs", align_bytes=64)
            nc.vector.quantize_mx(out=hq_t[e][:].bitcast(FP8X4), scales=hs_t[e][:], in_=hi_t[e][:].rearrange("p s d -> p (s d)"))

        def second(e):
            y_t[e] = psum.tile([P, C], F32, name="yp")
            nc.tensor.matmul_mx(
                out=y_t[e][:],
                lhsT=w2t[:, e].bitcast(FP4X4),
                lhsT_scale=s2[:, e],
                rhs=hq_t[e][:].bitcast(FP8X4),
                rhs_scale=hs_t[e][:],
                start=True,
                stop=True,
            )

        def keep(e):
            nc.scalar.copy(y[:, e * C : (e + 1) * C], y_t[e][:])

        groups = [(0, 1), (1, 1), (2, 2), (4, 2), (6, 2)]
        gather(*groups.pop(0))
        gather(*groups.pop(0))
        first(0)
        for e in range(E + 2):
            if groups and groups[0][0] <= e + 2:
                gather(*groups.pop(0))
            if e < E:
                gelu(e)
                mul(e)
                turn(e)
            if 0 <= e - 1 < E:
                lay(e - 1)
                quant(e - 1)
                second(e - 1)
            if 0 <= e - 2 < E:
                keep(e - 2)
            if e + 1 < E:
                first(e + 1)

        o1 = held.tile([P, T], F32, name="o1")
        o2 = held.tile([P, T], F32, name="o2")
        res = held.tile([P, T], F32, name="res")
        parts = ((0, 512), (512, T))
        for lo, hi in parts:
            sl, ls = slice(lo, hi), slice(lo // 16, hi // 16)
            nc.vector.tensor_tensor(o1[:, sl], y[:].indirect(pos1_t[:, ls]), gates[0][:, sl], MULT)
            nc.vector.tensor_tensor(o2[:, sl], y[:].indirect(pos2_t[:, ls]), gates[1][:, sl], MULT)
        for lo, hi in parts:
            sl = slice(lo, hi)
            nc.vector.tensor_tensor(res[:, sl], o1[:, sl], o2[:, sl], ADD)
            nc.sync.dma_start(out=out[:, sl], in_=res[:, sl])
